import numpy as np
import ml_dtypes


def mxq(x, axis, fmt="e4m3"):
    dtype, down = {"e4m3": (ml_dtypes.float8_e4m3fn, 7), "e5m2": (ml_dtypes.float8_e5m2, 14)}[fmt]
    v = np.moveaxis(np.asarray(x, np.float32).astype(ml_dtypes.bfloat16).astype(np.float64), axis, -1)
    blocks = v.reshape(v.shape[:-1] + (-1, 32))
    amax = np.abs(blocks).max(-1, keepdims=True)
    byte = np.maximum(np.where(amax > 0, np.frexp(amax)[1] - 1 + 127, 0) - down, 1)
    scale = np.exp2(byte - 127.0)
    codes = (blocks / scale).astype(np.float32).astype(dtype).astype(np.float64)
    return np.moveaxis((codes * scale).reshape(v.shape), -1, axis)


WIDE = False


def mx_kscale(k):
    if not WIDE:
        return np.ones(k)
    levels = np.array([10, -10, 5, -5, 0])
    if k % 512:
        return np.exp2(np.random.permutation(np.resize(levels, k // 32))).repeat(32)
    a = np.empty((k // 512, 16))
    for p in range(k // 512):
        a[p, :8] = np.random.permutation(np.resize(levels, 8))
        for g in range(8):
            far = levels[np.abs(levels - a[p, g]) >= 10]
            a[p, g + 8] = far[np.random.randint(len(far))]
    return np.exp2(a.ravel()).repeat(32)


def f64(x):
    return np.asarray(x).astype(np.float64)


def striped(idx):
    return np.tile(idx.reshape(-1, 16).T, (8, 1)).astype(np.uint16)


def unstriped(offs):
    return offs[:16].T.reshape(-1).astype(np.int64)


def pack_weight(w):
    k, n = w.shape
    w = f64(np.asarray(w, np.float32).astype(ml_dtypes.bfloat16)).reshape(k // 32, 32, n)
    amax = np.abs(w).max(1)
    byte = np.clip(np.where(amax > 0, np.frexp(amax)[1] - 1 + 127 - 7, 1), 1, 254)
    scaled = (w * np.exp2(127.0 - byte)[:, None, :]).reshape(k, n).astype(np.float32)
    words = np.ascontiguousarray(scaled.reshape(k // 512, 128, 4, n).transpose(0, 1, 3, 2)).astype(ml_dtypes.float8_e4m3fn).view(np.uint8)
    return words, np.ascontiguousarray(byte.astype(np.uint8).reshape(k // 512, 16, n))


def unpack_weight(words, scales):
    g, p, n, _ = words.shape
    vals = np.ascontiguousarray(words).view(ml_dtypes.float8_e4m3fn).astype(np.float64) * np.repeat(np.exp2(scales.astype(np.float64) - 127.0), 8, axis=1)[..., None]
    return vals.transpose(0, 1, 3, 2).reshape(g * 512, n)


K, T, S, N, H, W = 512, 2048, 512, 512, 512, 1024


def setup_inputs():
    n = np.random.standard_normal
    s = mx_kscale(K)[:, None]
    u = mx_kscale(H)
    packed_xT = pack_weight(n((K, T)) * s)
    return {
        "x_words": packed_xT[0],
        "x_scales": packed_xT[1],
        "w1": (n((K, H)) / np.sqrt(K) / s).astype(np.float32),
        "gn": (np.random.uniform(0.5, 1.5, (H, 1)) * u[:, None]).astype(np.float32),
        "w2": (n((H, N)) / np.sqrt(2 * H) / u[:, None]).astype(np.float32),
        "w3": (n((K, N)) / np.sqrt(2 * K) / s).astype(np.float32),
        "offs": striped(np.random.permutation(T)[:S]),
        "n1": striped(np.random.permutation(S)),
        "n2": striped(np.random.permutation(S)),
        "two": striped(np.random.permutation(T)[:S]),
        "n3": striped(np.random.randint(0, S, W)),
        "n4": striped(np.random.permutation(S)),
    }


def reference(x_words, x_scales, w1, gn, w2, w3, offs, n1, n2, two, n3, n4):
    xq = unpack_weight(x_words, x_scales)[:, unstriped(offs)]
    y = mxq(f64(w1), 0, "e4m3").T @ xq
    z = f64(gn) * ((y * y[:, unstriped(n1)]) * (np.tanh(y[:, unstriped(n2)])))
    x_two = unpack_weight(x_words, x_scales)[:, unstriped(two)]
    h = mxq(f64(w2), 0, "e4m3").T @ mxq(z, 0, "e4m3") + mxq(f64(w3), 0, "e4m3").T @ x_two
    mb = h[:, unstriped(n3)]
    mx = mb.reshape(N, S, 2).max(axis=2)
    st = h - mx
    return np.maximum(st, st[:, unstriped(n4)])

@@ -1,0 +1,237 @@
+from contextlib import ExitStack
+
+import concourse.mybir as mybir
+
+K, T, S, N, H, W = 512, 2048, 512, 512, 512, 1024
+FLOPS = 3 * 2 * 512 * 512 * 512
+
+F32 = mybir.dt.float32
+BF16 = mybir.dt.bfloat16
+I32 = mybir.dt.int32
+U32 = mybir.dt.uint32
+U16 = mybir.dt.uint16
+U8 = mybir.dt.uint8
+FP8X4 = mybir.dt.float8_e4m3fn_x4
+ALU = mybir.AluOpType
+ACT = mybir.ActivationFunctionType
+
+P = 128
+PACK = 4
+HALF = 256
+H_WIN = 544
+ST_WIN = 704
+COLS = HALF // 16
+
+
+def tile_picked_mixincubeghopm_none_p_kernel(
+    tc, x_words, x_scales, w1, gn, w2, w3, offs, n1, n2, two, n3, n4, out
+):
+    nc = tc.nc
+    with ExitStack() as ctx:
+        lists = ctx.enter_context(tc.tile_pool(name="lists", bufs=1))
+        keep = ctx.enter_context(tc.tile_pool(name="keep", bufs=1))
+        psum = ctx.enter_context(tc.psum_pool(name="psum", bufs=1))
+
+        def load_list(src, name):
+            tile = lists.tile(list(src.shape), U16, name=name)
+            nc.sync.dma_start(tile[:], src)
+            return tile
+
+        def piece(lst, i):
+            return lst[:, i * COLS : (i + 1) * COLS]
+
+        xs = keep.tile([P, T], U8, name="xs", align_bytes=64)
+        nc.gpsimd.memset(xs[:].bitcast(I32), 0)
+        offs_t = load_list(offs, "offs_t")
+        xw = keep.tile([P, T], U32, name="xw", align_bytes=64)
+        nc.sync.dma_start(xw[:].bitcast(I32), x_words[0].rearrange("p n t -> p (n t)").bitcast(I32))
+        for q in range(4):
+            nc.scalar.dma_start(xs[32 * q : 32 * q + 4, :].bitcast(I32), x_scales[0, 4 * q : 4 * q + 4, :].bitcast(I32))
+
+        def load_weight_half(w, a, name):
+            raw = keep.tile([P, PACK, HALF], F32, name=name, align_bytes=64)
+            nc.sync.dma_start(raw[:], w.rearrange("(p j) c -> p j c", j=PACK)[:, :, a * HALF : (a + 1) * HALF])
+            return raw
+
+        w1_raw = [load_weight_half(w1, a, f"w1_raw{a}") for a in range(2)]
+        two_t = load_list(two, "two_t")
+        gn_t = keep.tile([P, PACK], F32, name="gn_t", align_bytes=64)
+        nc.sync.dma_start(gn_t[:], gn.rearrange("(p t) o -> p (t o)", t=PACK))
+        n1_t = load_list(n1, "n1_t")
+        n2_t = load_list(n2, "n2_t")
+        w2_raw = keep.tile([P, PACK, N], F32, name="w2_raw", align_bytes=64)
+        nc.sync.dma_start(w2_raw[:], w2.rearrange("(p j) c -> p j c", j=PACK))
+        w3_raw = keep.tile([P, PACK, N], F32, name="w3_raw", align_bytes=64)
+        nc.sync.dma_start(w3_raw[:], w3.rearrange("(p j) c -> p j c", j=PACK))
+        n3_t = load_list(n3, "n3_t")
+        n4_t = load_list(n4, "n4_t")
+
+        xa_s = keep.tile([P, S], U8, name="xa_s", align_bytes=64)
+        xa_w = keep.tile([P, S], U32, name="xa_w", align_bytes=64)
+        xb_w = keep.tile([P, S], U32, name="xb_w", align_bytes=64)
+        nc.vector.tensor_copy(xa_s[:], xs[:].indirect(offs_t[:]))
+        nc.vector.tensor_copy(xa_w[:], xw[:].indirect(offs_t[:]))
+        nc.vector.tensor_copy(xb_w[:], xw[:].indirect(two_t[:]))
+
+        w1_g = keep.tile([P, PACK, P, PACK], BF16, name="w1_g", tag="w1_g", align_bytes=64)
+        for a in range(2):
+            src = w1_raw[a][:].rearrange("p j (m t) -> p m j t", t=PACK)
+            dst = w1_g[:, :, 64 * a : 64 * (a + 1), :].rearrange("p t m j -> p m j t")
+            if a == 0:
+                nc.scalar.copy(dst, src)
+            else:
+                nc.scalar.copy(dst[:, 0:24], src[:, 0:24])
+                nc.vector.tensor_copy(dst[:, 24:64], src[:, 24:64])
+        w1_c = keep.tile([P, PACK, P], U32, name="w1_c", align_bytes=64)
+        w1_s = keep.tile([P, PACK, P], U8, name="w1_s", align_bytes=64)
+        y_ps = [psum.tile([P, S], F32, name=f"y_ps{t}") for t in range(PACK)]
+        y_sb = [keep.tile([P, S], F32, name=f"y_sb{t}", align_bytes=64) for t in range(PACK)]
+        ty_sb = [keep.tile([P, S], F32, name=f"ty_sb{t}", align_bytes=64) for t in range(PACK)]
+        for t in range(PACK):
+            nc.vector.quantize_mx(
+                out=w1_c[:, t, :].bitcast(FP8X4), scales=w1_s[:, t, :], in_=w1_g[:, t].rearrange("p m j -> p (m j)")
+            )
+        for t in range(PACK):
+            nc.tensor.matmul_mx(
+                out=y_ps[t][:], lhsT=w1_c[:, t, :].bitcast(FP8X4), lhsT_scale=w1_s[:, t, :],
+                rhs=xa_w[:].bitcast(FP8X4), rhs_scale=xa_s[:], start=True, stop=True,
+            )
+        xb_s = keep.tile([P, S], U8, name="xb_s", tag="w1_g", align_bytes=64)
+        nc.vector.tensor_copy(xb_s[:], xs[:].indirect(two_t[:]))
+        for t in range(PACK):
+            nc.scalar.activation(ty_sb[t][:], y_ps[t][:], ACT.Tanh)
+            nc.scalar.copy(y_sb[t][:], y_ps[t][:])
+
+        def cast_weight(raw, a, name, engine):
+            g = keep.tile([P, HALF, PACK], BF16, name=name, align_bytes=64)
+            src = raw[:, :, a * HALF : (a + 1) * HALF].rearrange("p j (c i) -> p c j i", i=4)
+            dst = g[:].rearrange("p (c i) j -> p c j i", i=4)
+            if engine == "scalar":
+                nc.scalar.copy(dst, src)
+            else:
+                nc.vector.tensor_copy(dst, src)
+            return g
+
+        def quantize(g, name):
+            codes = keep.tile([P, HALF], U32, name=name + "_c", align_bytes=64)
+            scales = keep.tile([P, HALF], U8, name=name + "_s", align_bytes=64)
+            nc.vector.quantize_mx(out=codes[:].bitcast(FP8X4), scales=scales[:], in_=g[:].rearrange("p c j -> p (c j)"))
+            return codes, scales
+
+        h_ps = [psum.tile([P, S], F32, name=f"h_ps{m}") for m in range(4)]
+        h_sb = [keep.tile([P, H_WIN], F32, name=f"h_sb{m}", align_bytes=64) for m in range(4)]
+        st = [keep.tile([P, ST_WIN if m < 3 else S], F32, name=f"st{m}", align_bytes=64) for m in range(4)]
+        for m in range(4):
+            nc.gpsimd.memset(h_sb[m][:, S:H_WIN], 0.0)
+            if m < 3:
+                nc.gpsimd.memset(st[m][:, S:ST_WIN], 0.0)
+        z_q, w2_q, w3_q = [], [], []
+
+        def hidden(m, a):
+            cols = slice(a * HALF, (a + 1) * HALF)
+            mc = slice((m % 2) * P, (m % 2 + 1) * P)
+            c3, s3 = w3_q[m // 2]
+            c2, s2 = w2_q[m // 2]
+            zc, zs = z_q[a]
+            nc.tensor.matmul_mx(
+                out=h_ps[m][:, cols], lhsT=c3[:, mc].bitcast(FP8X4), lhsT_scale=s3[:, mc],
+                rhs=xb_w[:, cols].bitcast(FP8X4), rhs_scale=xb_s[:, cols], start=True, stop=False,
+            )
+            nc.tensor.matmul_mx(
+                out=h_ps[m][:, cols], lhsT=c2[:, mc].bitcast(FP8X4), lhsT_scale=s2[:, mc],
+                rhs=zc[:].bitcast(FP8X4), rhs_scale=zs[:], start=False, stop=True,
+            )
+
+        for a in range(2):
+            cols = slice(a * HALF, (a + 1) * HALF)
+            u = keep.tile([P, PACK, HALF], F32, name=f"u_{a}", align_bytes=64)
+            g2 = keep.tile([P, PACK, HALF], F32, name=f"g2_{a}", align_bytes=64)
+            for t in range(PACK):
+                g1 = keep.tile([P, HALF], F32, name=f"g1_{a}_{t}", align_bytes=64)
+                nc.scalar.activation(g1[:], y_sb[t][:].indirect(piece(n1_t, a)), ACT.Copy)
+                if a == 1 and t >= 2:
+                    nc.scalar.activation(g2[:, t, :], ty_sb[t][:].indirect(piece(n2_t, a)), ACT.Copy)
+                else:
+                    nc.vector.tensor_copy(g2[:, t, :], ty_sb[t][:].indirect(piece(n2_t, a)))
+                nc.vector.scalar_tensor_tensor(u[:, t, :], g1[:], gn_t[:, t : t + 1], y_ps[t][:, cols], ALU.mult, ALU.mult)
+            z_g = keep.tile([P, HALF, PACK], BF16, name=f"z_g{a}", align_bytes=64)
+            nc.vector.tensor_tensor(
+                z_g[:].rearrange("p (c i) t -> p c t i", i=4),
+                u[:].rearrange("p t (c i) -> p c t i", i=4),
+                g2[:].rearrange("p t (c i) -> p c t i", i=4),
+                ALU.mult,
+            )
+            if a == 0:
+                w2_g0 = cast_weight(w2_raw, 0, "w2_g0", "vector")
+                z_q.append(quantize(z_g, "z0"))
+                w3_g0 = cast_weight(w3_raw, 0, "w3_g0", "vector")
+                w2_q.append(quantize(w2_g0, "w2_0"))
+                w3_q.append(quantize(w3_g0, "w3_0"))
+                for m in range(2):
+                    hidden(m, 0)
+                nc.vector.tensor_copy(h_sb[0][:, cols], h_ps[0][:, cols])
+            else:
+                z_q.append(quantize(z_g, "z1"))
+        w2_g1 = cast_weight(w2_raw, 1, "w2_g1", "scalar")
+        w3_g1 = cast_weight(w3_raw, 1, "w3_g1", "scalar")
+        hidden(0, 1)
+        hidden(1, 1)
+        nc.vector.tensor_copy(h_sb[0][:, HALF:S], h_ps[0][:, HALF:S])
+        w2_q.append(quantize(w2_g1, "w2_1"))
+        w3_q.append(quantize(w3_g1, "w3_1"))
+        nc.vector.tensor_copy(h_sb[1][:, 0:S], h_ps[1][:])
+        for m in range(2, 4):
+            hidden(m, 0)
+            hidden(m, 1)
+            nc.vector.tensor_copy(h_sb[m][:, 0:S], h_ps[m][:])
+
+        mb = [keep.tile([P, W], F32, name=f"mb{m}", align_bytes=64) for m in range(4)]
+        mx = [keep.tile([P, S], F32, name=f"mx{m}", align_bytes=64) for m in range(4)]
+        sg = [keep.tile([P, S], F32, name=f"sg{m}", align_bytes=64) for m in range(4)]
+        res = [keep.tile([P, S], F32, name=f"res{m}", align_bytes=64) for m in range(4)]
+        whole = slice(0, S)
+        halves = [slice(0, HALF), slice(HALF, S)]
+
+        def members(m):
+            for a in range(2):
+                nc.scalar.activation(mb[m][:, a * S : (a + 1) * S], h_sb[m][:].indirect(n3_t[:, 32 * a : 32 * (a + 1)]), ACT.Copy)
+
+        def larger(m, cols):
+            pairs = mb[m][:, 2 * cols.start : 2 * cols.stop]
+            nc.vector.tensor_tensor(mx[m][:, cols], pairs[:, 0::2], pairs[:, 1::2], ALU.max)
+
+        def less(m, cols):
+            nc.vector.tensor_tensor(st[m][:, cols], h_ps[m][:, cols], mx[m][:, cols], ALU.subtract)
+
+        def fetch(m, cols, engine):
+            window = st[m][:].indirect(n4_t[:, cols.start // 16 : cols.stop // 16])
+            if engine == "scalar":
+                nc.scalar.activation(sg[m][:, cols], window, ACT.Copy)
+            else:
+                nc.vector.tensor_copy(sg[m][:, cols], window)
+
+        def finish(m, cols):
+            nc.vector.tensor_tensor(res[m][:, cols], st[m][:, cols], sg[m][:, cols], ALU.max)
+            nc.sync.dma_start(out[m * P : (m + 1) * P, cols], res[m][:, cols])
+
+        for m in range(4):
+            members(m)
+        larger(0, whole)
+        less(0, whole)
+        fetch(0, whole, "vector")
+        larger(1, whole)
+        finish(0, whole)
+        less(1, whole)
+        fetch(1, whole, "vector")
+        larger(2, whole)
+        finish(1, whole)
+        less(2, whole)
+        fetch(2, whole, "scalar")
+        for cols in halves:
+            larger(3, cols)
+        for cols in halves:
+            less(3, cols)
+        finish(2, whole)
+        for cols in halves:
+            fetch(3, cols, "scalar")
+            finish(3, cols)

@@ -18,6 +18,7 @@ ACT = mybir.ActivationFunctionType
 P = 128
 PACK = 4
 HALF = 256
+FIRST = 384
 H_WIN = 544
 ST_WIN = 704
 COLS = HALF // 16
@@ -41,12 +42,14 @@ def tile_picked_mixincubeghopm_none_p_kernel(
             return lst[:, i * COLS : (i + 1) * COLS]
 
         xs = keep.tile([P, T], U8, name="xs", align_bytes=64)
-        nc.gpsimd.memset(xs[:].bitcast(I32), 0)
+        for q in range(4):
+            rows = x_scales[0, 4 * q : 4 * q + 4, :].bitcast(I32)
+            queue = nc.sync if q % 2 == 0 else nc.scalar
+            queue.dma_start(xs[32 * q : 32 * q + 32, :].bitcast(I32), rows.unsqueeze(0).to_broadcast([8, 4, T // 4]))
         offs_t = load_list(offs, "offs_t")
+        two_t = load_list(two, "two_t")
         xw = keep.tile([P, T], U32, name="xw", align_bytes=64)
         nc.sync.dma_start(xw[:].bitcast(I32), x_words[0].rearrange("p n t -> p (n t)").bitcast(I32))
-        for q in range(4):
-            nc.scalar.dma_start(xs[32 * q : 32 * q + 4, :].bitcast(I32), x_scales[0, 4 * q : 4 * q + 4, :].bitcast(I32))
 
         def load_weight_half(w, a, name):
             raw = keep.tile([P, PACK, HALF], F32, name=name, align_bytes=64)
@@ -54,7 +57,6 @@ def tile_picked_mixincubeghopm_none_p_kernel(
             return raw
 
         w1_raw = [load_weight_half(w1, a, f"w1_raw{a}") for a in range(2)]
-        two_t = load_list(two, "two_t")
         gn_t = keep.tile([P, PACK], F32, name="gn_t", align_bytes=64)
         nc.sync.dma_start(gn_t[:], gn.rearrange("(p t) o -> p (t o)", t=PACK))
         n1_t = load_list(n1, "n1_t")
@@ -69,11 +71,13 @@ def tile_picked_mixincubeghopm_none_p_kernel(
         xa_s = keep.tile([P, S], U8, name="xa_s", align_bytes=64)
         xa_w = keep.tile([P, S], U32, name="xa_w", align_bytes=64)
         xb_w = keep.tile([P, S], U32, name="xb_w", align_bytes=64)
+        xb_s = keep.tile([P, S], U8, name="xb_s", align_bytes=64)
         nc.vector.tensor_copy(xa_s[:], xs[:].indirect(offs_t[:]))
+        nc.vector.tensor_copy(xb_s[:], xs[:].indirect(two_t[:]))
         nc.vector.tensor_copy(xa_w[:], xw[:].indirect(offs_t[:]))
         nc.vector.tensor_copy(xb_w[:], xw[:].indirect(two_t[:]))
 
-        w1_g = keep.tile([P, PACK, P, PACK], BF16, name="w1_g", tag="w1_g", align_bytes=64)
+        w1_g = keep.tile([P, PACK, P, PACK], BF16, name="w1_g", align_bytes=64)
         for a in range(2):
             src = w1_raw[a][:].rearrange("p j (m t) -> p m j t", t=PACK)
             dst = w1_g[:, :, 64 * a : 64 * (a + 1), :].rearrange("p t m j -> p m j t")
@@ -82,41 +86,37 @@ def tile_picked_mixincubeghopm_none_p_kernel(
             else:
                 nc.scalar.copy(dst[:, 0:24], src[:, 0:24])
                 nc.vector.tensor_copy(dst[:, 24:64], src[:, 24:64])
-        w1_c = keep.tile([P, PACK, P], U32, name="w1_c", align_bytes=64)
-        w1_s = keep.tile([P, PACK, P], U8, name="w1_s", align_bytes=64)
+        def quantize(g, width, name):
+            codes = keep.tile([P, width], U32, name=name + "_c", align_bytes=64)
+            scales = keep.tile([P, width], U8, name=name + "_s", align_bytes=64)
+            nc.vector.quantize_mx(out=codes[:].bitcast(FP8X4), scales=scales[:], in_=g.rearrange("p c j -> p (c j)"))
+            return codes, scales
+
+        def product(acc, weights, rows, tokens, cols, start, stop):
+            nc.tensor.matmul_mx(
+                out=acc, lhsT=weights[0][:, rows].bitcast(FP8X4), lhsT_scale=weights[1][:, rows],
+                rhs=tokens[0][:, cols].bitcast(FP8X4), rhs_scale=tokens[1][:, cols], start=start, stop=stop,
+            )
+
         y_ps = [psum.tile([P, S], F32, name=f"y_ps{t}") for t in range(PACK)]
         y_sb = [keep.tile([P, S], F32, name=f"y_sb{t}", align_bytes=64) for t in range(PACK)]
         ty_sb = [keep.tile([P, S], F32, name=f"ty_sb{t}", align_bytes=64) for t in range(PACK)]
+        w1_q = [quantize(w1_g[:, t], P, f"w1_{t}") for t in range(PACK)]
         for t in range(PACK):
-            nc.vector.quantize_mx(
-                out=w1_c[:, t, :].bitcast(FP8X4), scales=w1_s[:, t, :], in_=w1_g[:, t].rearrange("p m j -> p (m j)")
-            )
-        for t in range(PACK):
-            nc.tensor.matmul_mx(
-                out=y_ps[t][:], lhsT=w1_c[:, t, :].bitcast(FP8X4), lhsT_scale=w1_s[:, t, :],
-                rhs=xa_w[:].bitcast(FP8X4), rhs_scale=xa_s[:], start=True, stop=True,
-            )
-        xb_s = keep.tile([P, S], U8, name="xb_s", tag="w1_g", align_bytes=64)
-        nc.vector.tensor_copy(xb_s[:], xs[:].indirect(two_t[:]))
+            product(y_ps[t][:], w1_q[t], slice(0, P), (xa_w, xa_s), slice(0, S), True, True)
         for t in range(PACK):
             nc.scalar.activation(ty_sb[t][:], y_ps[t][:], ACT.Tanh)
             nc.scalar.copy(y_sb[t][:], y_ps[t][:])
 
-        def cast_weight(raw, a, name, engine):
-            g = keep.tile([P, HALF, PACK], BF16, name=name, align_bytes=64)
-            src = raw[:, :, a * HALF : (a + 1) * HALF].rearrange("p j (c i) -> p c j i", i=4)
-            dst = g[:].rearrange("p (c i) j -> p c j i", i=4)
-            if engine == "scalar":
-                nc.scalar.copy(dst, src)
-            else:
-                nc.vector.tensor_copy(dst, src)
+        def cast_weight(raw, name):
+            g = keep.tile([P, N, PACK], BF16, name=name, align_bytes=64)
+            for a in range(2):
+                cols = slice(a * HALF, (a + 1) * HALF)
+                nc.vector.tensor_copy(
+                    g[:, cols, :].rearrange("p (c i) j -> p c j i", i=4),
+                    raw[:, :, cols].rearrange("p j (c i) -> p c j i", i=4),
+                )
             return g
-
-        def quantize(g, name):
-            codes = keep.tile([P, HALF], U32, name=name + "_c", align_bytes=64)
-            scales = keep.tile([P, HALF], U8, name=name + "_s", align_bytes=64)
-            nc.vector.quantize_mx(out=codes[:].bitcast(FP8X4), scales=scales[:], in_=g[:].rearrange("p c j -> p (c j)"))
-            return codes, scales
 
         h_ps = [psum.tile([P, S], F32, name=f"h_ps{m}") for m in range(4)]
         h_sb = [keep.tile([P, H_WIN], F32, name=f"h_sb{m}", align_bytes=64) for m in range(4)]
@@ -125,65 +125,60 @@ def tile_picked_mixincubeghopm_none_p_kernel(
             nc.gpsimd.memset(h_sb[m][:, S:H_WIN], 0.0)
             if m < 3:
                 nc.gpsimd.memset(st[m][:, S:ST_WIN], 0.0)
-        z_q, w2_q, w3_q = [], [], []
 
-        def hidden(m, a):
-            cols = slice(a * HALF, (a + 1) * HALF)
-            mc = slice((m % 2) * P, (m % 2 + 1) * P)
-            c3, s3 = w3_q[m // 2]
-            c2, s2 = w2_q[m // 2]
-            zc, zs = z_q[a]
-            nc.tensor.matmul_mx(
-                out=h_ps[m][:, cols], lhsT=c3[:, mc].bitcast(FP8X4), lhsT_scale=s3[:, mc],
-                rhs=xb_w[:, cols].bitcast(FP8X4), rhs_scale=xb_s[:, cols], start=True, stop=False,
-            )
-            nc.tensor.matmul_mx(
-                out=h_ps[m][:, cols], lhsT=c2[:, mc].bitcast(FP8X4), lhsT_scale=s2[:, mc],
-                rhs=zc[:].bitcast(FP8X4), rhs_scale=zs[:], start=False, stop=True,
-            )
-
-        for a in range(2):
-            cols = slice(a * HALF, (a + 1) * HALF)
-            u = keep.tile([P, PACK, HALF], F32, name=f"u_{a}", align_bytes=64)
-            g2 = keep.tile([P, PACK, HALF], F32, name=f"g2_{a}", align_bytes=64)
+        def mixed(cols, on_scalar, name):
+            width = cols.stop - cols.start
+            entries = slice(cols.start // 16, cols.stop // 16)
+            u = keep.tile([P, PACK, width], F32, name=name + "_u", align_bytes=64)
+            g2 = keep.tile([P, PACK, width], F32, name=name + "_g2", align_bytes=64)
             for t in range(PACK):
-                g1 = keep.tile([P, HALF], F32, name=f"g1_{a}_{t}", align_bytes=64)
-                nc.scalar.activation(g1[:], y_sb[t][:].indirect(piece(n1_t, a)), ACT.Copy)
-                if a == 1 and t >= 2:
-                    nc.scalar.activation(g2[:, t, :], ty_sb[t][:].indirect(piece(n2_t, a)), ACT.Copy)
+                g1 = keep.tile([P, width], F32, name=f"{name}_g1_{t}", align_bytes=64)
+                nc.scalar.activation(g1[:], y_sb[t][:].indirect(n1_t[:, entries]), ACT.Copy)
+                if t in on_scalar:
+                    nc.scalar.activation(g2[:, t, :], ty_sb[t][:].indirect(n2_t[:, entries]), ACT.Copy)
                 else:
-                    nc.vector.tensor_copy(g2[:, t, :], ty_sb[t][:].indirect(piece(n2_t, a)))
+                    nc.vector.tensor_copy(g2[:, t, :], ty_sb[t][:].indirect(n2_t[:, entries]))
                 nc.vector.scalar_tensor_tensor(u[:, t, :], g1[:], gn_t[:, t : t + 1], y_ps[t][:, cols], ALU.mult, ALU.mult)
-            z_g = keep.tile([P, HALF, PACK], BF16, name=f"z_g{a}", align_bytes=64)
+            return u, g2
+
+        def rounded(u, g2, width, name):
+            z_g = keep.tile([P, width, PACK], BF16, name=name, align_bytes=64)
             nc.vector.tensor_tensor(
                 z_g[:].rearrange("p (c i) t -> p c t i", i=4),
                 u[:].rearrange("p t (c i) -> p c t i", i=4),
                 g2[:].rearrange("p t (c i) -> p c t i", i=4),
                 ALU.mult,
             )
-            if a == 0:
-                w2_g0 = cast_weight(w2_raw, 0, "w2_g0", "vector")
-                z_q.append(quantize(z_g, "z0"))
-                w3_g0 = cast_weight(w3_raw, 0, "w3_g0", "vector")
-                w2_q.append(quantize(w2_g0, "w2_0"))
-                w3_q.append(quantize(w3_g0, "w3_0"))
-                for m in range(2):
-                    hidden(m, 0)
-                nc.vector.tensor_copy(h_sb[0][:, cols], h_ps[0][:, cols])
-            else:
-                z_q.append(quantize(z_g, "z1"))
-        w2_g1 = cast_weight(w2_raw, 1, "w2_g1", "scalar")
-        w3_g1 = cast_weight(w3_raw, 1, "w3_g1", "scalar")
-        hidden(0, 1)
-        hidden(1, 1)
-        nc.vector.tensor_copy(h_sb[0][:, HALF:S], h_ps[0][:, HALF:S])
-        w2_q.append(quantize(w2_g1, "w2_1"))
-        w3_q.append(quantize(w3_g1, "w3_1"))
-        nc.vector.tensor_copy(h_sb[1][:, 0:S], h_ps[1][:])
-        for m in range(2, 4):
-            hidden(m, 0)
-            hidden(m, 1)
-            nc.vector.tensor_copy(h_sb[m][:, 0:S], h_ps[m][:])
+            return z_g
+
+        first, last = slice(0, FIRST), slice(FIRST, S)
+        xb = (xb_w, xb_s)
+        u0, g20 = mixed(first, (3,), "first")
+        w2_g = cast_weight(w2_raw, "w2_g")
+        w3_g = cast_weight(w3_raw, "w3_g")
+        w2_q = quantize(w2_g[:], N, "w2")
+        w3_q = quantize(w3_g[:], N, "w3")
+        z0_g = rounded(u0, g20, FIRST, "z0_g")
+        u1, g21 = mixed(last, (0, 1, 2, 3), "last")
+        z0_q = quantize(z0_g[:], FIRST, "z0")
+        runs = [slice(0, HALF), slice(HALF, FIRST)]
+        for m in range(4):
+            rows = slice(m * P, (m + 1) * P)
+            for i, cols in enumerate(runs):
+                product(h_ps[m][:, cols], w3_q, rows, xb, cols, i == 0, False)
+        for m in range(4):
+            rows = slice(m * P, (m + 1) * P)
+            for i, cols in enumerate(runs):
+                product(h_ps[m][:, cols], w2_q, rows, z0_q, cols, False, i == 1)
+        z1_g = rounded(u1, g21, S - FIRST, "z1_g")
+        z1_q = quantize(z1_g[:], S - FIRST, "z1")
+        for m in range(4):
+            nc.scalar.copy(h_sb[m][:, first], h_ps[m][:, first])
+        for m in range(4):
+            rows = slice(m * P, (m + 1) * P)
+            product(h_ps[m][:, last], w3_q, rows, xb, last, True, False)
+            product(h_ps[m][:, last], w2_q, rows, z1_q, slice(0, S - FIRST), False, True)
+            nc.vector.tensor_copy(h_sb[m][:, last], h_ps[m][:, last])
 
         mb = [keep.tile([P, W], F32, name=f"mb{m}", align_bytes=64) for m in range(4)]
         mx = [keep.tile([P, S], F32, name=f"mx{m}", align_bytes=64) for m in range(4)]
@@ -216,14 +211,17 @@ def tile_picked_mixincubeghopm_none_p_kernel(
 
         for m in range(4):
             members(m)
-        larger(0, whole)
-        less(0, whole)
+        for cols in halves:
+            larger(0, cols)
+            less(0, cols)
         fetch(0, whole, "vector")
-        larger(1, whole)
+        for cols in halves:
+            larger(1, cols)
         finish(0, whole)
         less(1, whole)
+        larger(2, halves[0])
         fetch(1, whole, "vector")
-        larger(2, whole)
+        larger(2, halves[1])
         finish(1, whole)
         less(2, whole)
         fetch(2, whole, "scalar")

@@ -2,7 +2,7 @@ from contextlib import ExitStack
 
 import concourse.mybir as mybir
 
-K, T, S, N, H, W = 512, 2048, 512, 512, 512, 1024
+T, S, N, W = 2048, 512, 512, 1024
 FLOPS = 3 * 2 * 512 * 512 * 512
 
 F32 = mybir.dt.float32
@@ -17,11 +17,14 @@ ACT = mybir.ActivationFunctionType
 
 P = 128
 PACK = 4
-HALF = 256
+BLOCKS = 4
+GROUP = 16
+RUN = 4
+HALF = S // 2
 FIRST = 384
-H_WIN = 544
-ST_WIN = 704
-COLS = HALF // 16
+W1_SCALAR_SHARE = 24
+H_WINDOW = 544
+ST_WINDOW = 704
 
 
 def tile_picked_mixincubeghopm_none_p_kernel(
@@ -33,203 +36,214 @@ def tile_picked_mixincubeghopm_none_p_kernel(
         keep = ctx.enter_context(tc.tile_pool(name="keep", bufs=1))
         psum = ctx.enter_context(tc.psum_pool(name="psum", bufs=1))
 
+        def sbuf(shape, dtype, name, tag=None):
+            return keep.tile(shape, dtype, name=name, tag=tag or name, align_bytes=64)
+
         def load_list(src, name):
             tile = lists.tile(list(src.shape), U16, name=name)
             nc.sync.dma_start(tile[:], src)
             return tile
 
-        def piece(lst, i):
-            return lst[:, i * COLS : (i + 1) * COLS]
+        def entries(lst, cols):
+            return lst[:, cols.start // GROUP : cols.stop // GROUP]
 
-        xs = keep.tile([P, T], U8, name="xs", align_bytes=64)
+        def load_weight(w, cols, name):
+            raw = sbuf([P, PACK, cols.stop - cols.start], F32, name)
+            nc.sync.dma_start(raw[:], w.rearrange("(p j) c -> p j c", j=PACK)[:, :, cols])
+            return raw
+
+        whole = slice(0, S)
+        halves = [slice(0, HALF), slice(HALF, S)]
+        first, last = slice(0, FIRST), slice(FIRST, S)
+
+        x_s = sbuf([P, T], U8, "x_s")
         for q in range(4):
             rows = x_scales[0, 4 * q : 4 * q + 4, :].bitcast(I32)
             queue = nc.sync if q % 2 == 0 else nc.scalar
-            queue.dma_start(xs[32 * q : 32 * q + 32, :].bitcast(I32), rows.unsqueeze(0).to_broadcast([8, 4, T // 4]))
+            queue.dma_start(x_s[32 * q : 32 * q + 32, :].bitcast(I32), rows.unsqueeze(0).to_broadcast([8, 4, T // 4]))
         offs_t = load_list(offs, "offs_t")
         two_t = load_list(two, "two_t")
-        xw = keep.tile([P, T], U32, name="xw", align_bytes=64)
-        nc.sync.dma_start(xw[:].bitcast(I32), x_words[0].rearrange("p n t -> p (n t)").bitcast(I32))
-
-        def load_weight_half(w, a, name):
-            raw = keep.tile([P, PACK, HALF], F32, name=name, align_bytes=64)
-            nc.sync.dma_start(raw[:], w.rearrange("(p j) c -> p j c", j=PACK)[:, :, a * HALF : (a + 1) * HALF])
-            return raw
-
-        w1_raw = [load_weight_half(w1, a, f"w1_raw{a}") for a in range(2)]
-        gn_t = keep.tile([P, PACK], F32, name="gn_t", align_bytes=64)
+        x_w = sbuf([P, T], U32, "x_w")
+        nc.sync.dma_start(x_w[:].bitcast(I32), x_words[0].rearrange("p n t -> p (n t)").bitcast(I32))
+        w1_raw = [load_weight(w1, cols, f"w1_raw{a}") for a, cols in enumerate(halves)]
+        gn_t = sbuf([P, PACK], F32, "gn_t")
         nc.sync.dma_start(gn_t[:], gn.rearrange("(p t) o -> p (t o)", t=PACK))
         n1_t = load_list(n1, "n1_t")
         n2_t = load_list(n2, "n2_t")
-        w2_raw = keep.tile([P, PACK, N], F32, name="w2_raw", align_bytes=64)
-        nc.sync.dma_start(w2_raw[:], w2.rearrange("(p j) c -> p j c", j=PACK))
-        w3_raw = keep.tile([P, PACK, N], F32, name="w3_raw", align_bytes=64)
-        nc.sync.dma_start(w3_raw[:], w3.rearrange("(p j) c -> p j c", j=PACK))
+        w2_raw = load_weight(w2, whole, "w2_raw")
+        w3_raw = load_weight(w3, whole, "w3_raw")
         n3_t = load_list(n3, "n3_t")
         n4_t = load_list(n4, "n4_t")
 
-        xa_s = keep.tile([P, S], U8, name="xa_s", align_bytes=64)
-        xa_w = keep.tile([P, S], U32, name="xa_w", align_bytes=64)
-        xb_w = keep.tile([P, S], U32, name="xb_w", align_bytes=64)
-        xb_s = keep.tile([P, S], U8, name="xb_s", align_bytes=64)
-        nc.vector.tensor_copy(xa_s[:], xs[:].indirect(offs_t[:]))
-        nc.vector.tensor_copy(xb_s[:], xs[:].indirect(two_t[:]))
-        nc.vector.tensor_copy(xa_w[:], xw[:].indirect(offs_t[:]))
-        nc.vector.tensor_copy(xb_w[:], xw[:].indirect(two_t[:]))
+        xa_s = sbuf([P, S], U8, "xa_s")
+        xa_w = sbuf([P, S], U32, "xa_w")
+        xb_w = sbuf([P, S], U32, "xb_w")
+        xb_s = sbuf([P, S], U8, "xb_s")
+        nc.vector.tensor_copy(xa_s[:], x_s[:].indirect(offs_t[:]))
+        nc.vector.tensor_copy(xb_s[:], x_s[:].indirect(two_t[:]))
+        nc.vector.tensor_copy(xa_w[:], x_w[:].indirect(offs_t[:]))
+        nc.vector.tensor_copy(xb_w[:], x_w[:].indirect(two_t[:]))
+        xa, xb = (xa_w, xa_s), (xb_w, xb_s)
 
-        w1_g = keep.tile([P, PACK, P, PACK], BF16, name="w1_g", align_bytes=64)
-        for a in range(2):
-            src = w1_raw[a][:].rearrange("p j (m t) -> p m j t", t=PACK)
-            dst = w1_g[:, :, 64 * a : 64 * (a + 1), :].rearrange("p t m j -> p m j t")
-            if a == 0:
-                nc.scalar.copy(dst, src)
-            else:
-                nc.scalar.copy(dst[:, 0:24], src[:, 0:24])
-                nc.vector.tensor_copy(dst[:, 24:64], src[:, 24:64])
-        def quantize(g, width, name):
-            codes = keep.tile([P, width], U32, name=name + "_c", align_bytes=64)
-            scales = keep.tile([P, width], U8, name=name + "_s", align_bytes=64)
-            nc.vector.quantize_mx(out=codes[:].bitcast(FP8X4), scales=scales[:], in_=g.rearrange("p c j -> p (c j)"))
-            return codes, scales
+        def quantize(grouped, width, name):
+            words = sbuf([P, width], U32, name + "_w")
+            scales = sbuf([P, width], U8, name + "_s")
+            nc.vector.quantize_mx(
+                out=words[:].bitcast(FP8X4), scales=scales[:], in_=grouped.rearrange("p c j -> p (c j)")
+            )
+            return words, scales
 
         def product(acc, weights, rows, tokens, cols, start, stop):
             nc.tensor.matmul_mx(
-                out=acc, lhsT=weights[0][:, rows].bitcast(FP8X4), lhsT_scale=weights[1][:, rows],
-                rhs=tokens[0][:, cols].bitcast(FP8X4), rhs_scale=tokens[1][:, cols], start=start, stop=stop,
+                out=acc,
+                lhsT=weights[0][:, rows].bitcast(FP8X4),
+                lhsT_scale=weights[1][:, rows],
+                rhs=tokens[0][:, cols].bitcast(FP8X4),
+                rhs_scale=tokens[1][:, cols],
+                start=start,
+                stop=stop,
             )
 
+        w1_g = sbuf([P, PACK, P, PACK], BF16, "w1_g")
+        per_half = P // 2
+        for a in range(2):
+            src = w1_raw[a][:].rearrange("p j (m t) -> p m j t", t=PACK)
+            dst = w1_g[:, :, per_half * a : per_half * (a + 1), :].rearrange("p t m j -> p m j t")
+            if a == 0:
+                nc.scalar.copy(dst, src)
+            else:
+                nc.scalar.copy(dst[:, 0:W1_SCALAR_SHARE], src[:, 0:W1_SCALAR_SHARE])
+                nc.vector.tensor_copy(dst[:, W1_SCALAR_SHARE:per_half], src[:, W1_SCALAR_SHARE:per_half])
         y_ps = [psum.tile([P, S], F32, name=f"y_ps{t}") for t in range(PACK)]
-        y_sb = [keep.tile([P, S], F32, name=f"y_sb{t}", align_bytes=64) for t in range(PACK)]
-        ty_sb = [keep.tile([P, S], F32, name=f"ty_sb{t}", align_bytes=64) for t in range(PACK)]
+        y_sb = [sbuf([P, S], F32, f"y_sb{t}") for t in range(PACK)]
+        tanh_sb = [sbuf([P, S], F32, f"tanh_sb{t}") for t in range(PACK)]
         w1_q = [quantize(w1_g[:, t], P, f"w1_{t}") for t in range(PACK)]
         for t in range(PACK):
-            product(y_ps[t][:], w1_q[t], slice(0, P), (xa_w, xa_s), slice(0, S), True, True)
+            product(y_ps[t][:], w1_q[t], slice(0, P), xa, whole, True, True)
         for t in range(PACK):
-            nc.scalar.activation(ty_sb[t][:], y_ps[t][:], ACT.Tanh)
-            nc.scalar.copy(y_sb[t][:], y_ps[t][:])
+            if t == 1:
+                nc.vector.tensor_copy(y_sb[t][:], y_ps[t][:])
+            nc.scalar.activation(tanh_sb[t][:], y_ps[t][:], ACT.Tanh)
+            if t != 1:
+                nc.scalar.copy(y_sb[t][:], y_ps[t][:])
 
-        def cast_weight(raw, name):
-            g = keep.tile([P, N, PACK], BF16, name=name, align_bytes=64)
-            for a in range(2):
-                cols = slice(a * HALF, (a + 1) * HALF)
-                nc.vector.tensor_copy(
-                    g[:, cols, :].rearrange("p (c i) j -> p c j i", i=4),
-                    raw[:, :, cols].rearrange("p j (c i) -> p c j i", i=4),
-                )
-            return g
+        h_ps = [psum.tile([P, FIRST], F32, name=f"h_ps{m}") for m in range(BLOCKS)]
+        h_sb = [sbuf([P, H_WINDOW], F32, f"h_sb{m}") for m in range(BLOCKS)]
+        st = [sbuf([P, ST_WINDOW if m < BLOCKS - 1 else S], F32, f"st{m}") for m in range(BLOCKS)]
+        for m in range(BLOCKS):
+            nc.gpsimd.memset(h_sb[m][:, S:H_WINDOW], 0.0)
+            if m < BLOCKS - 1:
+                nc.gpsimd.memset(st[m][:, S:ST_WINDOW], 0.0)
 
-        h_ps = [psum.tile([P, S], F32, name=f"h_ps{m}") for m in range(4)]
-        h_sb = [keep.tile([P, H_WIN], F32, name=f"h_sb{m}", align_bytes=64) for m in range(4)]
-        st = [keep.tile([P, ST_WIN if m < 3 else S], F32, name=f"st{m}", align_bytes=64) for m in range(4)]
-        for m in range(4):
-            nc.gpsimd.memset(h_sb[m][:, S:H_WIN], 0.0)
-            if m < 3:
-                nc.gpsimd.memset(st[m][:, S:ST_WIN], 0.0)
-
-        def mixed(cols, on_scalar, name):
-            width = cols.stop - cols.start
-            entries = slice(cols.start // 16, cols.stop // 16)
-            u = keep.tile([P, PACK, width], F32, name=name + "_u", align_bytes=64)
-            g2 = keep.tile([P, PACK, width], F32, name=name + "_g2", align_bytes=64)
-            for t in range(PACK):
-                g1 = keep.tile([P, width], F32, name=f"{name}_g1_{t}", align_bytes=64)
-                nc.scalar.activation(g1[:], y_sb[t][:].indirect(n1_t[:, entries]), ACT.Copy)
-                if t in on_scalar:
-                    nc.scalar.activation(g2[:, t, :], ty_sb[t][:].indirect(n2_t[:, entries]), ACT.Copy)
-                else:
-                    nc.vector.tensor_copy(g2[:, t, :], ty_sb[t][:].indirect(n2_t[:, entries]))
-                nc.vector.scalar_tensor_tensor(u[:, t, :], g1[:], gn_t[:, t : t + 1], y_ps[t][:, cols], ALU.mult, ALU.mult)
-            return u, g2
-
-        def rounded(u, g2, width, name):
-            z_g = keep.tile([P, width, PACK], BF16, name=name, align_bytes=64)
-            nc.vector.tensor_tensor(
-                z_g[:].rearrange("p (c i) t -> p c t i", i=4),
-                u[:].rearrange("p t (c i) -> p c t i", i=4),
-                g2[:].rearrange("p t (c i) -> p c t i", i=4),
-                ALU.mult,
+        def round_weight(raw, name):
+            grouped = sbuf([P, N, PACK], BF16, name)
+            nc.vector.tensor_copy(
+                grouped[:].rearrange("p (c i) j -> p c j i", i=RUN), raw[:].rearrange("p j (c i) -> p c j i", i=RUN)
             )
-            return z_g
+            return grouped
 
-        first, last = slice(0, FIRST), slice(FIRST, S)
-        xb = (xb_w, xb_s)
-        u0, g20 = mixed(first, (3,), "first")
-        w2_g = cast_weight(w2_raw, "w2_g")
-        w3_g = cast_weight(w3_raw, "w3_g")
+        w2_g = round_weight(w2_raw, "w2_g")
+        w3_g = round_weight(w3_raw, "w3_g")
         w2_q = quantize(w2_g[:], N, "w2")
         w3_q = quantize(w3_g[:], N, "w3")
-        z0_g = rounded(u0, g20, FIRST, "z0_g")
-        u1, g21 = mixed(last, (0, 1, 2, 3), "last")
-        z0_q = quantize(z0_g[:], FIRST, "z0")
-        runs = [slice(0, HALF), slice(HALF, FIRST)]
-        for m in range(4):
-            rows = slice(m * P, (m + 1) * P)
-            for i, cols in enumerate(runs):
-                product(h_ps[m][:, cols], w3_q, rows, xb, cols, i == 0, False)
-        for m in range(4):
-            rows = slice(m * P, (m + 1) * P)
-            for i, cols in enumerate(runs):
-                product(h_ps[m][:, cols], w2_q, rows, z0_q, cols, False, i == 1)
-        z1_g = rounded(u1, g21, S - FIRST, "z1_g")
-        z1_q = quantize(z1_g[:], S - FIRST, "z1")
-        for m in range(4):
-            nc.scalar.copy(h_sb[m][:, first], h_ps[m][:, first])
-        for m in range(4):
-            rows = slice(m * P, (m + 1) * P)
-            product(h_ps[m][:, last], w3_q, rows, xb, last, True, False)
-            product(h_ps[m][:, last], w2_q, rows, z1_q, slice(0, S - FIRST), False, True)
-            nc.vector.tensor_copy(h_sb[m][:, last], h_ps[m][:, last])
 
-        mb = [keep.tile([P, W], F32, name=f"mb{m}", align_bytes=64) for m in range(4)]
-        mx = [keep.tile([P, S], F32, name=f"mx{m}", align_bytes=64) for m in range(4)]
-        sg = [keep.tile([P, S], F32, name=f"sg{m}", align_bytes=64) for m in range(4)]
-        res = [keep.tile([P, S], F32, name=f"res{m}", align_bytes=64) for m in range(4)]
-        whole = slice(0, S)
-        halves = [slice(0, HALF), slice(HALF, S)]
+        def z_factors(cols, tanh_on_scalar, name, pair_tag):
+            width = cols.stop - cols.start
+            pair = sbuf([P, PACK, width], F32, name + "_pair", pair_tag)
+            looked_tanh = sbuf([P, PACK, width], F32, name + "_tanh")
+            for t in range(PACK):
+                looked_y = sbuf([P, width], F32, f"{name}_y{t}")
+                nc.scalar.activation(looked_y[:], y_sb[t][:].indirect(entries(n1_t, cols)), ACT.Copy)
+                if t not in tanh_on_scalar:
+                    nc.vector.tensor_copy(looked_tanh[:, t, :], tanh_sb[t][:].indirect(entries(n2_t, cols)))
+                nc.vector.scalar_tensor_tensor(
+                    pair[:, t, :], looked_y[:], gn_t[:, t : t + 1], y_ps[t][:, cols], ALU.mult, ALU.mult
+                )
+            for t in tanh_on_scalar:
+                nc.scalar.activation(looked_tanh[:, t, :], tanh_sb[t][:].indirect(entries(n2_t, cols)), ACT.Copy)
+            return pair, looked_tanh
+
+        def z_rounded(pair, looked_tanh, width, name):
+            grouped = sbuf([P, width, PACK], BF16, name)
+            nc.vector.tensor_tensor(
+                grouped[:].rearrange("p (c i) t -> p c t i", i=RUN),
+                pair[:].rearrange("p t (c i) -> p c t i", i=RUN),
+                looked_tanh[:].rearrange("p t (c i) -> p c t i", i=RUN),
+                ALU.mult,
+            )
+            return grouped
+
+        factors = z_factors(first, (3,), "first", "first_pair")
+        z_first_q = quantize(z_rounded(*factors, FIRST, "z_first_g")[:], FIRST, "z_first")
+        factors = z_factors(last, (0, 1, 2, 3), "last", "first_tanh")
+
+        runs = [slice(0, HALF), slice(HALF, FIRST)]
+        block_rows = [slice(m * P, (m + 1) * P) for m in range(BLOCKS)]
+        for m in range(BLOCKS):
+            for i, cols in enumerate(runs):
+                product(h_ps[m][:, cols], w3_q, block_rows[m], xb, cols, i == 0, False)
+        for m in range(BLOCKS):
+            for i, cols in enumerate(runs):
+                product(h_ps[m][:, cols], w2_q, block_rows[m], z_first_q, cols, False, i == 1)
+        z_last_q = quantize(z_rounded(*factors, S - FIRST, "z_last_g")[:], S - FIRST, "z_last")
+        for m in range(BLOCKS):
+            nc.scalar.copy(h_sb[m][:, first], h_ps[m][:])
+        for m in range(BLOCKS):
+            h_last = psum.tile([P, S - FIRST], F32, name=f"h_last{m}", tag=f"y_ps{m}")
+            product(h_last[:], w3_q, block_rows[m], xb, last, True, False)
+            product(h_last[:], w2_q, block_rows[m], z_last_q, slice(0, S - FIRST), False, True)
+            nc.vector.tensor_copy(h_sb[m][:, last], h_last[:])
+
+        mb = [sbuf([P, W], F32, f"mb{m}") for m in range(BLOCKS)]
+        mx = {}
+        looked_st = [sbuf([P, S], F32, f"looked_st{m}") for m in range(BLOCKS)]
+        result = [sbuf([P, S], F32, f"result{m}") for m in range(BLOCKS)]
 
         def members(m):
-            for a in range(2):
-                nc.scalar.activation(mb[m][:, a * S : (a + 1) * S], h_sb[m][:].indirect(n3_t[:, 32 * a : 32 * (a + 1)]), ACT.Copy)
+            for part in (slice(0, S), slice(S, W)):
+                nc.scalar.activation(mb[m][:, part], h_sb[m][:].indirect(entries(n3_t, part)), ACT.Copy)
 
         def larger(m, cols):
+            if m not in mx:
+                mx[m] = sbuf([P, S], F32, f"mx{m}", f"mx{max(m, 1)}")
             pairs = mb[m][:, 2 * cols.start : 2 * cols.stop]
             nc.vector.tensor_tensor(mx[m][:, cols], pairs[:, 0::2], pairs[:, 1::2], ALU.max)
 
         def less(m, cols):
-            nc.vector.tensor_tensor(st[m][:, cols], h_ps[m][:, cols], mx[m][:, cols], ALU.subtract)
+            nc.vector.tensor_tensor(st[m][:, cols], h_sb[m][:, cols], mx[m][:, cols], ALU.subtract)
 
-        def fetch(m, cols, engine):
-            window = st[m][:].indirect(n4_t[:, cols.start // 16 : cols.stop // 16])
-            if engine == "scalar":
-                nc.scalar.activation(sg[m][:, cols], window, ACT.Copy)
-            else:
-                nc.vector.tensor_copy(sg[m][:, cols], window)
+        def fetch_on_vector(m, cols):
+            nc.vector.tensor_copy(looked_st[m][:, cols], st[m][:].indirect(entries(n4_t, cols)))
+
+        def fetch_on_scalar(m, cols):
+            nc.scalar.activation(looked_st[m][:, cols], st[m][:].indirect(entries(n4_t, cols)), ACT.Copy)
 
         def finish(m, cols):
-            nc.vector.tensor_tensor(res[m][:, cols], st[m][:, cols], sg[m][:, cols], ALU.max)
-            nc.sync.dma_start(out[m * P : (m + 1) * P, cols], res[m][:, cols])
+            nc.vector.tensor_tensor(result[m][:, cols], st[m][:, cols], looked_st[m][:, cols], ALU.max)
+            nc.sync.dma_start(out[block_rows[m], cols], result[m][:, cols])
 
-        for m in range(4):
+        left, right = halves
+        for m in range(BLOCKS):
             members(m)
         for cols in halves:
             larger(0, cols)
             less(0, cols)
-        fetch(0, whole, "vector")
+        fetch_on_vector(0, whole)
         for cols in halves:
             larger(1, cols)
         finish(0, whole)
         less(1, whole)
-        larger(2, halves[0])
-        fetch(1, whole, "vector")
-        larger(2, halves[1])
-        finish(1, whole)
+        larger(2, left)
+        fetch_on_vector(1, whole)
+        larger(2, right)
+        larger(3, left)
         less(2, whole)
-        fetch(2, whole, "scalar")
-        for cols in halves:
-            larger(3, cols)
-        for cols in halves:
-            less(3, cols)
+        fetch_on_scalar(2, whole)
+        less(3, left)
+        larger(3, right)
+        finish(1, whole)
+        less(3, right)
         finish(2, whole)
         for cols in halves:
-            fetch(3, cols, "scalar")
+            fetch_on_scalar(3, cols)
             finish(3, cols)

from contextlib import ExitStack

import concourse.mybir as mybir

T, S, N, W = 2048, 512, 512, 1024
FLOPS = 3 * 2 * 512 * 512 * 512

F32 = mybir.dt.float32
BF16 = mybir.dt.bfloat16
I32 = mybir.dt.int32
U32 = mybir.dt.uint32
U16 = mybir.dt.uint16
U8 = mybir.dt.uint8
FP8X4 = mybir.dt.float8_e4m3fn_x4
ALU = mybir.AluOpType
ACT = mybir.ActivationFunctionType

P = 128
PACK = 4
BLOCKS = 4
GROUP = 16
RUN = 4
HALF = S // 2
FIRST = 384
W1_SCALAR_SHARE = 24
H_WINDOW = 544
ST_WINDOW = 704


def tile_picked_mixincubeghopm_none_p_kernel(
    tc, x_words, x_scales, w1, gn, w2, w3, offs, n1, n2, two, n3, n4, out
):
    nc = tc.nc
    with ExitStack() as ctx:
        lists = ctx.enter_context(tc.tile_pool(name="lists", bufs=1))
        keep = ctx.enter_context(tc.tile_pool(name="keep", bufs=1))
        psum = ctx.enter_context(tc.psum_pool(name="psum", bufs=1))

        def sbuf(shape, dtype, name, tag=None):
            return keep.tile(shape, dtype, name=name, tag=tag or name, align_bytes=64)

        def load_list(src, name):
            tile = lists.tile(list(src.shape), U16, name=name)
            nc.sync.dma_start(tile[:], src)
            return tile

        def entries(lst, cols):
            return lst[:, cols.start // GROUP : cols.stop // GROUP]

        def load_weight(w, cols, name):
            raw = sbuf([P, PACK, cols.stop - cols.start], F32, name)
            nc.sync.dma_start(raw[:], w.rearrange("(p j) c -> p j c", j=PACK)[:, :, cols])
            return raw

        whole = slice(0, S)
        halves = [slice(0, HALF), slice(HALF, S)]
        first, last = slice(0, FIRST), slice(FIRST, S)

        x_s = sbuf([P, T], U8, "x_s")
        for q in range(4):
            rows = x_scales[0, 4 * q : 4 * q + 4, :].bitcast(I32)
            queue = nc.sync if q % 2 == 0 else nc.scalar
            queue.dma_start(x_s[32 * q : 32 * q + 32, :].bitcast(I32), rows.unsqueeze(0).to_broadcast([8, 4, T // 4]))
        offs_t = load_list(offs, "offs_t")
        two_t = load_list(two, "two_t")
        x_w = sbuf([P, T], U32, "x_w")
        nc.sync.dma_start(x_w[:].bitcast(I32), x_words[0].rearrange("p n t -> p (n t)").bitcast(I32))
        w1_raw = [load_weight(w1, cols, f"w1_raw{a}") for a, cols in enumerate(halves)]
        gn_t = sbuf([P, PACK], F32, "gn_t")
        nc.sync.dma_start(gn_t[:], gn.rearrange("(p t) o -> p (t o)", t=PACK))
        n1_t = load_list(n1, "n1_t")
        n2_t = load_list(n2, "n2_t")
        w2_raw = load_weight(w2, whole, "w2_raw")
        w3_raw = load_weight(w3, whole, "w3_raw")
        n3_t = load_list(n3, "n3_t")
        n4_t = load_list(n4, "n4_t")

        xa_s = sbuf([P, S], U8, "xa_s")
        xa_w = sbuf([P, S], U32, "xa_w")
        xb_w = sbuf([P, S], U32, "xb_w")
        xb_s = sbuf([P, S], U8, "xb_s")
        nc.vector.tensor_copy(xa_s[:], x_s[:].indirect(offs_t[:]))
        nc.vector.tensor_copy(xb_s[:], x_s[:].indirect(two_t[:]))
        nc.vector.tensor_copy(xa_w[:], x_w[:].indirect(offs_t[:]))
        nc.vector.tensor_copy(xb_w[:], x_w[:].indirect(two_t[:]))
        xa, xb = (xa_w, xa_s), (xb_w, xb_s)

        def quantize(grouped, width, name):
            words = sbuf([P, width], U32, name + "_w")
            scales = sbuf([P, width], U8, name + "_s")
            nc.vector.quantize_mx(
                out=words[:].bitcast(FP8X4), scales=scales[:], in_=grouped.rearrange("p c j -> p (c j)")
            )
            return words, scales

        def product(acc, weights, rows, tokens, cols, start, stop):
            nc.tensor.matmul_mx(
                out=acc,
                lhsT=weights[0][:, rows].bitcast(FP8X4),
                lhsT_scale=weights[1][:, rows],
                rhs=tokens[0][:, cols].bitcast(FP8X4),
                rhs_scale=tokens[1][:, cols],
                start=start,
                stop=stop,
            )

        w1_g = sbuf([P, PACK, P, PACK], BF16, "w1_g")
        per_half = P // 2
        for a in range(2):
            src = w1_raw[a][:].rearrange("p j (m t) -> p m j t", t=PACK)
            dst = w1_g[:, :, per_half * a : per_half * (a + 1), :].rearrange("p t m j -> p m j t")
            if a == 0:
                nc.scalar.copy(dst, src)
            else:
                nc.scalar.copy(dst[:, 0:W1_SCALAR_SHARE], src[:, 0:W1_SCALAR_SHARE])
                nc.vector.tensor_copy(dst[:, W1_SCALAR_SHARE:per_half], src[:, W1_SCALAR_SHARE:per_half])
        y_ps = [psum.tile([P, S], F32, name=f"y_ps{t}") for t in range(PACK)]
        y_sb = [sbuf([P, S], F32, f"y_sb{t}") for t in range(PACK)]
        tanh_sb = [sbuf([P, S], F32, f"tanh_sb{t}") for t in range(PACK)]
        w1_q = [quantize(w1_g[:, t], P, f"w1_{t}") for t in range(PACK)]
        for t in range(PACK):
            product(y_ps[t][:], w1_q[t], slice(0, P), xa, whole, True, True)
        for t in range(PACK):
            if t == 1:
                nc.vector.tensor_copy(y_sb[t][:], y_ps[t][:])
            nc.scalar.activation(tanh_sb[t][:], y_ps[t][:], ACT.Tanh)
            if t != 1:
                nc.scalar.copy(y_sb[t][:], y_ps[t][:])

        h_ps = [psum.tile([P, FIRST], F32, name=f"h_ps{m}") for m in range(BLOCKS)]
        h_sb = [sbuf([P, H_WINDOW], F32, f"h_sb{m}") for m in range(BLOCKS)]
        st = [sbuf([P, ST_WINDOW if m < BLOCKS - 1 else S], F32, f"st{m}") for m in range(BLOCKS)]
        for m in range(BLOCKS):
            nc.gpsimd.memset(h_sb[m][:, S:H_WINDOW], 0.0)
            if m < BLOCKS - 1:
                nc.gpsimd.memset(st[m][:, S:ST_WINDOW], 0.0)

        def round_weight(raw, name):
            grouped = sbuf([P, N, PACK], BF16, name)
            nc.vector.tensor_copy(
                grouped[:].rearrange("p (c i) j -> p c j i", i=RUN), raw[:].rearrange("p j (c i) -> p c j i", i=RUN)
            )
            return grouped

        w2_g = round_weight(w2_raw, "w2_g")
        w3_g = round_weight(w3_raw, "w3_g")
        w2_q = quantize(w2_g[:], N, "w2")
        w3_q = quantize(w3_g[:], N, "w3")

        def z_factors(cols, tanh_on_scalar, name, pair_tag):
            width = cols.stop - cols.start
            pair = sbuf([P, PACK, width], F32, name + "_pair", pair_tag)
            looked_tanh = sbuf([P, PACK, width], F32, name + "_tanh")
            for t in range(PACK):
                looked_y = sbuf([P, width], F32, f"{name}_y{t}")
                nc.scalar.activation(looked_y[:], y_sb[t][:].indirect(entries(n1_t, cols)), ACT.Copy)
                if t not in tanh_on_scalar:
                    nc.vector.tensor_copy(looked_tanh[:, t, :], tanh_sb[t][:].indirect(entries(n2_t, cols)))
                nc.vector.scalar_tensor_tensor(
                    pair[:, t, :], looked_y[:], gn_t[:, t : t + 1], y_ps[t][:, cols], ALU.mult, ALU.mult
                )
            for t in tanh_on_scalar:
                nc.scalar.activation(looked_tanh[:, t, :], tanh_sb[t][:].indirect(entries(n2_t, cols)), ACT.Copy)
            return pair, looked_tanh

        def z_rounded(pair, looked_tanh, width, name):
            grouped = sbuf([P, width, PACK], BF16, name)
            nc.vector.tensor_tensor(
                grouped[:].rearrange("p (c i) t -> p c t i", i=RUN),
                pair[:].rearrange("p t (c i) -> p c t i", i=RUN),
                looked_tanh[:].rearrange("p t (c i) -> p c t i", i=RUN),
                ALU.mult,
            )
            return grouped

        factors = z_factors(first, (3,), "first", "first_pair")
        z_first_q = quantize(z_rounded(*factors, FIRST, "z_first_g")[:], FIRST, "z_first")
        factors = z_factors(last, (0, 1, 2, 3), "last", "first_tanh")

        runs = [slice(0, HALF), slice(HALF, FIRST)]
        block_rows = [slice(m * P, (m + 1) * P) for m in range(BLOCKS)]
        for m in range(BLOCKS):
            for i, cols in enumerate(runs):
                product(h_ps[m][:, cols], w3_q, block_rows[m], xb, cols, i == 0, False)
        for m in range(BLOCKS):
            for i, cols in enumerate(runs):
                product(h_ps[m][:, cols], w2_q, block_rows[m], z_first_q, cols, False, i == 1)
        z_last_q = quantize(z_rounded(*factors, S - FIRST, "z_last_g")[:], S - FIRST, "z_last")
        for m in range(BLOCKS):
            nc.scalar.copy(h_sb[m][:, first], h_ps[m][:])
        for m in range(BLOCKS):
            h_last = psum.tile([P, S - FIRST], F32, name=f"h_last{m}", tag=f"y_ps{m}")
            product(h_last[:], w3_q, block_rows[m], xb, last, True, False)
            product(h_last[:], w2_q, block_rows[m], z_last_q, slice(0, S - FIRST), False, True)
            nc.vector.tensor_copy(h_sb[m][:, last], h_last[:])

        mb = [sbuf([P, W], F32, f"mb{m}") for m in range(BLOCKS)]
        mx = {}
        looked_st = [sbuf([P, S], F32, f"looked_st{m}") for m in range(BLOCKS)]
        result = [sbuf([P, S], F32, f"result{m}") for m in range(BLOCKS)]

        def members(m):
            for part in (slice(0, S), slice(S, W)):
                nc.scalar.activation(mb[m][:, part], h_sb[m][:].indirect(entries(n3_t, part)), ACT.Copy)

        def larger(m, cols):
            if m not in mx:
                mx[m] = sbuf([P, S], F32, f"mx{m}", f"mx{max(m, 1)}")
            pairs = mb[m][:, 2 * cols.start : 2 * cols.stop]
            nc.vector.tensor_tensor(mx[m][:, cols], pairs[:, 0::2], pairs[:, 1::2], ALU.max)

        def less(m, cols):
            nc.vector.tensor_tensor(st[m][:, cols], h_sb[m][:, cols], mx[m][:, cols], ALU.subtract)

        def fetch_on_vector(m, cols):
            nc.vector.tensor_copy(looked_st[m][:, cols], st[m][:].indirect(entries(n4_t, cols)))

        def fetch_on_scalar(m, cols):
            nc.scalar.activation(looked_st[m][:, cols], st[m][:].indirect(entries(n4_t, cols)), ACT.Copy)

        def finish(m, cols):
            nc.vector.tensor_tensor(result[m][:, cols], st[m][:, cols], looked_st[m][:, cols], ALU.max)
            nc.sync.dma_start(out[block_rows[m], cols], result[m][:, cols])

        left, right = halves
        for m in range(BLOCKS):
            members(m)
        for cols in halves:
            larger(0, cols)
            less(0, cols)
        fetch_on_vector(0, whole)
        for cols in halves:
            larger(1, cols)
        finish(0, whole)
        less(1, whole)
        larger(2, left)
        fetch_on_vector(1, whole)
        larger(2, right)
        larger(3, left)
        less(2, whole)
        fetch_on_scalar(2, whole)
        less(3, left)
        larger(3, right)
        finish(1, whole)
        less(3, right)
        finish(2, whole)
        for cols in halves:
            fetch_on_scalar(3, cols)
            finish(3, cols)
